import numpy as np
import ml_dtypes


def mxq(x, axis, fmt="e4m3"):
    dtype, down = {"e4m3": (ml_dtypes.float8_e4m3fn, 7), "e5m2": (ml_dtypes.float8_e5m2, 14)}[fmt]
    v = np.moveaxis(np.asarray(x, np.float32).astype(ml_dtypes.bfloat16).astype(np.float64), axis, -1)
    blocks = v.reshape(v.shape[:-1] + (-1, 32))
    amax = np.abs(blocks).max(-1, keepdims=True)
    byte = np.maximum(np.where(amax > 0, np.frexp(amax)[1] - 1 + 127, 0) - down, 1)
    scale = np.exp2(byte - 127.0)
    codes = (blocks / scale).astype(np.float32).astype(dtype).astype(np.float64)
    return np.moveaxis((codes * scale).reshape(v.shape), -1, axis)


WIDE = False


def mx_kscale(k):
    if not WIDE:
        return np.ones(k)
    levels = np.array([30, -30])
    if k % 512:
        return np.exp2(np.random.permutation(np.resize(levels, k // 32))).repeat(32)
    a = np.empty((k // 512, 16))
    for p in range(k // 512):
        a[p, :8] = np.random.permutation(np.resize(levels, 8))
        for g in range(8):
            far = levels[np.abs(levels - a[p, g]) >= 10]
            a[p, g + 8] = far[np.random.randint(len(far))]
    return np.exp2(a.ravel()).repeat(32)


def f64(x):
    return np.asarray(x).astype(np.float64)


def striped(idx):
    return np.tile(np.asarray(idx).reshape(-1, 16).T, (8, 1)).astype(np.uint16)


def unstriped(offs):
    return offs[:16].T.reshape(-1).astype(np.int64)


E2M1 = np.array([0.0, 0.5, 1.0, 1.5, 2.0, 3.0, 4.0, 6.0, -0.0, -0.5, -1.0, -1.5, -2.0, -3.0, -4.0, -6.0])


def pack_weight(w, fmt):
    k, n = w.shape
    w = f64(np.asarray(w, np.float32).astype(ml_dtypes.bfloat16)).reshape(k // 32, 32, n)
    amax = np.abs(w).max(1)
    if fmt == "e4m3":
        byte = np.frexp(amax)[1] - 1 + 127 - 7
    else:
        mant, ex = np.frexp(amax / 6.0)
        byte = np.where(mant > 0.5, ex, ex - 1) + 127
    byte = np.clip(np.where(amax > 0, byte, 1), 1, 254)
    scaled = (w * np.exp2(127.0 - byte)[:, None, :]).reshape(k, n).astype(np.float32)
    by_word = np.ascontiguousarray(scaled.reshape(k // 512, 128, 4, n).transpose(0, 1, 3, 2))
    if fmt == "e4m3":
        words = by_word.astype(ml_dtypes.float8_e4m3fn).view(np.uint8)
    else:
        c = by_word.astype(ml_dtypes.float4_e2m1fn).view(np.uint8) & 0xF
        words = (c[..., 0::2] | (c[..., 1::2] << 4)).reshape(k // 512, 128, 2 * n)
    return np.ascontiguousarray(words), np.ascontiguousarray(byte.astype(np.uint8).reshape(k // 512, 16, n))


def unpack_weight(words, scales, fmt):
    g, _, n = scales.shape
    words = np.ascontiguousarray(words).reshape(g, 128, n, -1)
    if fmt == "e4m3":
        vals = words.view(ml_dtypes.float8_e4m3fn).astype(np.float64)
    else:
        nib = np.empty((g, 128, n, 4), np.uint8)
        nib[..., 0::2] = words & 0xF
        nib[..., 1::2] = words >> 4
        vals = E2M1[nib]
    vals = vals * np.repeat(np.exp2(scales.astype(np.float64) - 127.0), 8, axis=1)[..., None]
    return vals.transpose(0, 1, 3, 2).reshape(g * 512, n)


def sigmoid(v):
    return 1.0 / (1.0 + np.exp(-v))


K, T, Z, J, R, C, O, N, E = 512, 1024, 1024, 256, 512, 512, 256, 256, 1024


def setup_inputs():
    n = np.random.standard_normal
    idx = np.random.permutation(T)[:J]
    idx2 = np.random.permutation(Z)[:J]
    idx3 = np.random.permutation(C)[:J]
    idx4 = np.random.permutation(C)[:J]
    idx5 = np.random.permutation(C)[:O]
    idx6 = np.random.permutation(C)[:O]
    idx7 = np.random.permutation(E)[:O]
    fk = mx_kscale(K)
    fr = mx_kscale(R)
    xtp = pack_weight(n((K, T)) / fk[:, None], "e2m1")
    xop = pack_weight(n((K, Z)) / fk[:, None], "e4m3")
    wp = pack_weight(n((K, R)) * 1 / np.sqrt(K) * fk[:, None] * fr, "e4m3")
    wbp = pack_weight(n((R, N)) * 1 / np.sqrt(R) / fr[:, None], "e2m1")
    return {
        "xt_words": xtp[0],
        "xt_scales": xtp[1],
        "xo_words": xop[0],
        "xo_scales": xop[1],
        "w_words": wp[0],
        "w_scales": wp[1],
        "wb_words": wbp[0],
        "wb_scales": wbp[1],
        "tz": (n((N, E))).astype(np.float32),
        "so": (np.random.uniform(0.6, 1.6, (N, 1))).astype(np.float32),
        "bo": (np.random.uniform(-1.0, 1.0, (N, 1))).astype(np.float32),
        "offs": striped(idx),
        "offs2": striped(idx2),
        "offs3": striped(idx3),
        "offs4": striped(idx4),
        "offs5": striped(idx5),
        "offs6": striped(idx6),
        "offs7": striped(idx7),
    }


def reference(xt_words, xt_scales, xo_words, xo_scales, w_words, w_scales, wb_words, wb_scales, tz, so, bo, offs, offs2, offs3, offs4, offs5, offs6, offs7):
    idx = unstriped(offs)
    idx2 = unstriped(offs2)
    idx3 = unstriped(offs3)
    idx4 = unstriped(offs4)
    idx5 = unstriped(offs5)
    idx6 = unstriped(offs6)
    idx7 = unstriped(offs7)
    xtu = unpack_weight(xt_words, xt_scales, "e2m1")
    xou = unpack_weight(xo_words, xo_scales, "e4m3")
    wu = unpack_weight(w_words, w_scales, "e4m3")
    wbu = unpack_weight(wb_words, wb_scales, "e2m1")
    xtidxg = xtu[:, idx]
    a = wu.T @ xtidxg
    xoidx2g = xou[:, idx2]
    b = wu.T @ xoidx2g
    pw = np.zeros((R, C))
    pw[:, idx3] = a
    pv = np.zeros((R, C))
    pv[:, idx4] = b
    hid = np.abs(pw[:, idx5] - pv[:, idx6])
    hidq = mxq(hid, 0, "e5m2")
    p = wbu.T @ hidq
    y = p * sigmoid(f64(tz)[:, idx7] * f64(so) + f64(bo))
    return y

@@ -1,0 +1,199 @@
+from contextlib import ExitStack
+
+import concourse.mybir as mybir
+
+K, T, Z, J, R, C, O, N, E = 512, 1024, 1024, 256, 512, 512, 256, 256, 1024
+FLOPS = 2 * (2 * K * R * J + R * N * O)
+
+F32 = mybir.dt.float32
+BF16 = mybir.dt.bfloat16
+I32 = mybir.dt.int32
+U32 = mybir.dt.uint32
+U16 = mybir.dt.uint16
+U8 = mybir.dt.uint8
+E4M3 = mybir.dt.float8_e4m3fn_x4
+E5M2 = mybir.dt.float8_e5m2_x4
+E2M1 = mybir.dt.float4_e2m1fn_x4
+ACT = mybir.ActivationFunctionType
+ALU = mybir.AluOpType
+
+P = 128
+PACK = 4
+HALF = O // 2
+
+
+def tile_list_oneforboth_twoboards_one_finalgate_kernel(
+    tc, xt_words, xt_scales, xo_words, xo_scales, w_words, w_scales, wb_words, wb_scales,
+    tz, so, bo, offs, offs2, offs3, offs4, offs5, offs6, offs7, out,
+):
+    nc = tc.nc
+    with ExitStack() as ctx:
+        keep = ctx.enter_context(tc.tile_pool(name="keep", bufs=1))
+        psum = ctx.enter_context(tc.psum_pool(name="psum", bufs=1))
+
+        def sb(name, shape, dtype, tag=None):
+            return keep.tile(shape, dtype, name=name, tag=tag or name, align_bytes=64)
+
+        def load_list(name, src):
+            lst = sb(name, [P, J // 16], U16)
+            nc.sync.dma_start(lst[:], src)
+            return lst
+
+        def load_scales(name, src, cols, queues):
+            plane = sb(name, [P, cols], U8)
+            for q, queue in enumerate(queues):
+                rows = src[0, 4 * q : 4 * q + 4, :].bitcast(I32)
+                queue.dma_start(
+                    plane[32 * q : 32 * q + 32, :].bitcast(I32), rows.unsqueeze(0).to_broadcast([8, 4, cols // 4])
+                )
+            return plane
+
+        l_xt = load_list("l_xt", offs)
+        w_raw = sb("w_raw", [P, R], U32)
+        nc.sync.dma_start(w_raw[:].bitcast(I32), w_words[0].rearrange("p c t -> p (c t)").bitcast(I32))
+        xt_w = sb("xt_w", [P, T], U16)
+        nc.sync.dma_start(xt_w[:].bitcast(I32), xt_words[0].bitcast(I32))
+        w_sc = load_scales("w_sc", w_scales, R, [nc.scalar] * 4)
+        xt_sc = load_scales("xt_sc", xt_scales, T, [nc.sync] + [nc.gpsimd] * 3)
+        l_xo = load_list("l_xo", offs2)
+        xo_w = sb("xo_w", [P, Z], U32)
+        nc.sync.dma_start(xo_w[:].bitcast(I32), xo_words[0].rearrange("p c t -> p (c t)").bitcast(I32))
+        xo_sc = load_scales("xo_sc", xo_scales, Z, [nc.scalar] * 4)
+        l_pw_put = load_list("l_pw_put", offs3)
+        l_pv_put = load_list("l_pv_put", offs4)
+        l_pw_get = load_list("l_pw_get", offs5)
+        l_pv_get = load_list("l_pv_get", offs6)
+        l_tz = load_list("l_tz", offs7)
+        slope = sb("slope", [P, 2], F32)
+        offset = sb("offset", [P, 2], F32)
+        with nc.allow_non_contiguous_dma(reason="one value a partition"):
+            nc.gpsimd.dma_start(slope[:], so.rearrange("(h p) o -> p (h o)", p=P))
+            nc.gpsimd.dma_start(offset[:], bo.rearrange("(h p) o -> p (h o)", p=P))
+        tz_sb = [sb("tz%d" % h, [P, E], F32) for h in range(2)]
+        nc.sync.dma_start(tz_sb[0][:], tz[0:P, :])
+        wb_sc = load_scales("wb_sc", wb_scales, N, [nc.sync] * 4)
+        wb_w = sb("wb_w", [P, 2 * N], U8)
+        nc.sync.dma_start(wb_w[:].bitcast(I32), wb_words[0].bitcast(I32))
+        nc.sync.dma_start(tz_sb[1][:], tz[P : 2 * P, :])
+
+        warm_in = sb("warm_in", [P, 1], F32)
+        warm_out = sb("warm_out", [P, 1], F32)
+        nc.vector.memset(warm_in[:], 0.0)
+        nc.scalar.activation(out=warm_out[:], in_=warm_in[:], func=ACT.Sigmoid)
+        pw = [sb("pw%d" % t, [P, C], F32) for t in range(PACK)]
+        pv = [sb("pv%d" % t, [P, C], F32) for t in range(PACK)]
+        for board in pw:
+            nc.vector.memset(board[:], 0.0)
+        for board in pv:
+            nc.gpsimd.memset(board[:], 0.0)
+
+        w_deal = sb("w_deal", [P, PACK, P], U32)
+        w_sc_deal = sb("w_sc_deal", [P, PACK, P], U8)
+        nc.vector.tensor_copy(w_deal[:].rearrange("p t m -> p m t"), w_raw[:].rearrange("p (m t) -> p m t", t=PACK))
+        nc.vector.tensor_copy(w_sc_deal[:].rearrange("p t m -> p m t"), w_sc[:].rearrange("p (m t) -> p m t", t=PACK))
+
+        xt_g = sb("xt_g", [P, J], U16)
+        xt_sc_g = sb("xt_sc_g", [P, J], U8)
+        nc.vector.tensor_copy(xt_g[:], xt_w[:].indirect(l_xt[:]))
+        nc.vector.tensor_copy(xt_sc_g[:], xt_sc[:].indirect(l_xt[:]))
+
+        gate = sb("gate", [P, 2, O], F32)
+
+        def look(h):
+            nc.scalar.activation(
+                out=gate[:, h, :], in_=tz_sb[h][:].indirect(l_tz[:]), func=ACT.Sigmoid,
+                bias=offset[:, h : h + 1], scale=slope[:, h : h + 1],
+            )
+
+        def first_stage(acc, t, words, plane):
+            nc.tensor.matmul_mx(
+                out=acc, lhsT=w_deal[:, t, :].bitcast(E4M3), lhsT_scale=w_sc_deal[:, t, :],
+                rhs=words, rhs_scale=plane[:], start=True, stop=True,
+            )
+
+        a0_ps = psum.tile([P, J], F32, name="a0_ps")
+        a1_ps = psum.tile([P, J], F32, name="a1_ps")
+        a23_ps = psum.tile([P, 2, J], F32, name="a23_ps")
+        for t, acc in enumerate([a0_ps[:], a1_ps[:], a23_ps[:, 0, :], a23_ps[:, 1, :]]):
+            first_stage(acc, t, xt_g[:].bitcast(E2M1), xt_sc_g)
+
+        xo_g = sb("xo_g", [P, J], U32)
+        xo_sc_g = sb("xo_sc_g", [P, J], U8)
+        nc.vector.tensor_copy(xo_sc_g[:], xo_sc[:].indirect(l_xo[:]))
+        nc.vector.tensor_copy(xo_g[:], xo_w[:].indirect(l_xo[:]))
+        b01_ps = psum.tile([P, 2, J], F32, name="b01_ps")
+        b23_ps = psum.tile([P, 2, J], F32, name="b23_ps")
+        for t, acc in enumerate([b01_ps[:, 0, :], b01_ps[:, 1, :], b23_ps[:, 0, :], b23_ps[:, 1, :]]):
+            first_stage(acc, t, xo_g[:].bitcast(E4M3), xo_sc_g)
+
+        a_sb = sb("a_sb", [P, PACK, J], F32)
+        b_sb = sb("b_sb", [P, PACK, J], F32)
+        got_w = sb("got_w", [P, PACK, O], F32)
+        diff = sb("diff", [P, PACK, O], F32)
+
+        def put_s(board, lst, src):
+            nc.scalar.activation(out=board[:].indirect(lst[:]), in_=src, func=ACT.Copy)
+
+        def put_v(board, lst, src):
+            nc.vector.tensor_copy(board[:].indirect(lst[:]), src)
+
+        def get_w(t):
+            nc.scalar.activation(out=got_w[:, t, :], in_=pw[t][:].indirect(l_pw_get[:]), func=ACT.Copy)
+
+        def get_diff(t, lo, hi):
+            nc.vector.tensor_tensor(
+                diff[:, t, lo:hi], pv[t][:].indirect(l_pv_get[:, lo // 16 : hi // 16]), got_w[:, t, lo:hi], ALU.subtract
+            )
+
+        nc.scalar.copy(a_sb[:, 0, :], a0_ps[:])
+        put_s(pw[0], l_pw_put, a_sb[:, 0, :])
+        a1_sb = sb("a1_sb", [P, J], F32, tag="xo_w")
+        nc.vector.tensor_copy(a1_sb[:], a1_ps[:])
+        put_v(pw[1], l_pw_put, a1_sb[:])
+        nc.scalar.copy(a_sb[:, 2:4, :], a23_ps[:])
+        get_w(0)
+        nc.vector.tensor_copy(b_sb[:, 0:2, :], b01_ps[:])
+        put_s(pw[2], l_pw_put, a_sb[:, 2, :])
+        put_v(pw[3], l_pw_put, a_sb[:, 3, :])
+        nc.scalar.copy(b_sb[:, 2:4, :], b23_ps[:])
+        put_v(pv[1], l_pv_put, b_sb[:, 1, :])
+        put_s(pv[0], l_pv_put, b_sb[:, 0, :])
+        put_v(pv[3], l_pv_put, b_sb[:, 3, :])
+        get_w(1)
+        put_s(pv[2], l_pv_put, b_sb[:, 2, :])
+        get_diff(0, 0, O)
+        get_diff(1, 0, O)
+        get_w(3)
+        get_w(2)
+        get_diff(3, 0, O)
+        look(0)
+        get_diff(2, 0, HALF)
+        get_diff(2, HALF, O)
+
+        out_v = out.rearrange("(h p) o -> p h o", p=P)
+        p_banks = []
+        for u in range(2):
+            cols = slice(u * HALF, (u + 1) * HALF)
+            hid = sb("hid%d" % u, [P, HALF * PACK], BF16, tag="tz0" if u == 0 else None)
+            nc.scalar.activation(
+                out=hid[:].rearrange("p (c i t) -> p c t i", i=4, t=PACK),
+                in_=diff[:, :, cols].rearrange("p t (c i) -> p c t i", i=4),
+                func=ACT.Abs,
+            )
+            hid_w = sb("hid_w%d" % u, [P, HALF], U32)
+            hid_sc = sb("hid_sc%d" % u, [P, HALF], U8)
+            nc.vector.quantize_mx(out=hid_w[:].bitcast(E5M2), scales=hid_sc[:], in_=hid[:])
+            p_ps = psum.tile([P, 2, HALF], F32, name="p_ps%d" % u)
+            for h in range(2):
+                nc.tensor.matmul_mx(
+                    out=p_ps[:, h, :], lhsT=wb_w[:, 2 * P * h : 2 * P * (h + 1)].bitcast(E2M1),
+                    lhsT_scale=wb_sc[:, P * h : P * (h + 1)],
+                    rhs=hid_w[:].bitcast(E5M2), rhs_scale=hid_sc[:], start=True, stop=True,
+                )
+            p_banks.append(p_ps)
+        look(1)
+        for u, p_ps in enumerate(p_banks):
+            cols = slice(u * HALF, (u + 1) * HALF)
+            res = sb("res%d" % u, [P, 2, HALF], F32)
+            nc.vector.tensor_tensor(res[:], p_ps[:], gate[:, :, cols], ALU.mult)
+            nc.sync.dma_start(out_v[:, :, cols], res[:])

@@ -39,29 +39,34 @@ def tile_list_oneforboth_twoboards_one_finalgate_kernel(
             nc.sync.dma_start(lst[:], src)
             return lst
 
-        def load_scales(name, src, cols, queues):
-            plane = sb(name, [P, cols], U8)
-            for q, queue in enumerate(queues):
-                rows = src[0, 4 * q : 4 * q + 4, :].bitcast(I32)
-                queue.dma_start(
-                    plane[32 * q : 32 * q + 32, :].bitcast(I32), rows.unsqueeze(0).to_broadcast([8, 4, cols // 4])
-                )
-            return plane
+        def load_scale_rows(plane, src, q, queue):
+            rows = src[0, 4 * q : 4 * q + 4, :].bitcast(I32)
+            queue.dma_start(
+                plane[32 * q : 32 * q + 32, :].bitcast(I32), rows.unsqueeze(0).to_broadcast([8] + list(rows.shape))
+            )
 
         l_xt = load_list("l_xt", offs)
+        xt_sc = sb("xt_sc", [P, T], U8)
+        w_sc = sb("w_sc", [P, R], U8)
+        xo_sc = sb("xo_sc", [P, Z], U8)
+        wb_sc = sb("wb_sc", [P, N], U8)
+        for q in range(4):
+            load_scale_rows(xt_sc, xt_scales, q, nc.scalar)
+        load_scale_rows(w_sc, w_scales, 0, nc.sync)
         w_raw = sb("w_raw", [P, R], U32)
         nc.sync.dma_start(w_raw[:].bitcast(I32), w_words[0].rearrange("p c t -> p (c t)").bitcast(I32))
         xt_w = sb("xt_w", [P, T], U16)
         nc.sync.dma_start(xt_w[:].bitcast(I32), xt_words[0].bitcast(I32))
-        w_sc = load_scales("w_sc", w_scales, R, [nc.scalar] * 4)
-        xt_sc = load_scales("xt_sc", xt_scales, T, [nc.sync] + [nc.gpsimd] * 3)
+        for q, queue in [(1, nc.sync), (2, nc.scalar), (3, nc.sync)]:
+            load_scale_rows(w_sc, w_scales, q, queue)
+        for q, queue in enumerate([nc.scalar, nc.scalar, nc.gpsimd, nc.gpsimd]):
+            load_scale_rows(xo_sc, xo_scales, q, queue)
         l_xo = load_list("l_xo", offs2)
         xo_w = sb("xo_w", [P, Z], U32)
         nc.sync.dma_start(xo_w[:].bitcast(I32), xo_words[0].rearrange("p c t -> p (c t)").bitcast(I32))
-        xo_sc = load_scales("xo_sc", xo_scales, Z, [nc.scalar] * 4)
         l_pw_put = load_list("l_pw_put", offs3)
-        l_pv_put = load_list("l_pv_put", offs4)
         l_pw_get = load_list("l_pw_get", offs5)
+        l_pv_put = load_list("l_pv_put", offs4)
         l_pv_get = load_list("l_pv_get", offs6)
         l_tz = load_list("l_tz", offs7)
         slope = sb("slope", [P, 2], F32)
@@ -71,7 +76,8 @@ def tile_list_oneforboth_twoboards_one_finalgate_kernel(
             nc.gpsimd.dma_start(offset[:], bo.rearrange("(h p) o -> p (h o)", p=P))
         tz_sb = [sb("tz%d" % h, [P, E], F32) for h in range(2)]
         nc.sync.dma_start(tz_sb[0][:], tz[0:P, :])
-        wb_sc = load_scales("wb_sc", wb_scales, N, [nc.sync] * 4)
+        for q in range(4):
+            load_scale_rows(wb_sc, wb_scales, q, nc.sync)
         wb_w = sb("wb_w", [P, 2 * N], U8)
         nc.sync.dma_start(wb_w[:].bitcast(I32), wb_words[0].bitcast(I32))
         nc.sync.dma_start(tz_sb[1][:], tz[P : 2 * P, :])
@@ -81,21 +87,18 @@ def tile_list_oneforboth_twoboards_one_finalgate_kernel(
         nc.vector.memset(warm_in[:], 0.0)
         nc.scalar.activation(out=warm_out[:], in_=warm_in[:], func=ACT.Sigmoid)
         pw = [sb("pw%d" % t, [P, C], F32) for t in range(PACK)]
-        pv = [sb("pv%d" % t, [P, C], F32) for t in range(PACK)]
         for board in pw:
             nc.vector.memset(board[:], 0.0)
-        for board in pv:
-            nc.gpsimd.memset(board[:], 0.0)
 
         w_deal = sb("w_deal", [P, PACK, P], U32)
         w_sc_deal = sb("w_sc_deal", [P, PACK, P], U8)
         nc.vector.tensor_copy(w_deal[:].rearrange("p t m -> p m t"), w_raw[:].rearrange("p (m t) -> p m t", t=PACK))
-        nc.vector.tensor_copy(w_sc_deal[:].rearrange("p t m -> p m t"), w_sc[:].rearrange("p (m t) -> p m t", t=PACK))
 
         xt_g = sb("xt_g", [P, J], U16)
         xt_sc_g = sb("xt_sc_g", [P, J], U8)
         nc.vector.tensor_copy(xt_g[:], xt_w[:].indirect(l_xt[:]))
         nc.vector.tensor_copy(xt_sc_g[:], xt_sc[:].indirect(l_xt[:]))
+        nc.vector.tensor_copy(w_sc_deal[:].rearrange("p t m -> p m t"), w_sc[:].rearrange("p (m t) -> p m t", t=PACK))
 
         gate = sb("gate", [P, 2, O], F32)
 
@@ -119,8 +122,8 @@ def tile_list_oneforboth_twoboards_one_finalgate_kernel(
 
         xo_g = sb("xo_g", [P, J], U32)
         xo_sc_g = sb("xo_sc_g", [P, J], U8)
-        nc.vector.tensor_copy(xo_sc_g[:], xo_sc[:].indirect(l_xo[:]))
         nc.vector.tensor_copy(xo_g[:], xo_w[:].indirect(l_xo[:]))
+        nc.vector.tensor_copy(xo_sc_g[:], xo_sc[:].indirect(l_xo[:]))
         b01_ps = psum.tile([P, 2, J], F32, name="b01_ps")
         b23_ps = psum.tile([P, 2, J], F32, name="b23_ps")
         for t, acc in enumerate([b01_ps[:, 0, :], b01_ps[:, 1, :], b23_ps[:, 0, :], b23_ps[:, 1, :]]):
@@ -145,11 +148,16 @@ def tile_list_oneforboth_twoboards_one_finalgate_kernel(
                 diff[:, t, lo:hi], pv[t][:].indirect(l_pv_get[:, lo // 16 : hi // 16]), got_w[:, t, lo:hi], ALU.subtract
             )
 
+        pv = [sb("pv%d" % t, [P, C], F32, tag=tag) for t, tag in enumerate(["xo_w", "w_sc", "xo_sc", "xt_g"])]
+        for board in pv:
+            nc.gpsimd.memset(board[:], 0.0)
+        def get_w_v(t):
+            nc.vector.tensor_copy(got_w[:, t, :], pw[t][:].indirect(l_pw_get[:]))
+
         nc.scalar.copy(a_sb[:, 0, :], a0_ps[:])
+        nc.scalar.copy(a_sb[:, 1, :], a1_ps[:])
         put_s(pw[0], l_pw_put, a_sb[:, 0, :])
-        a1_sb = sb("a1_sb", [P, J], F32, tag="xo_w")
-        nc.vector.tensor_copy(a1_sb[:], a1_ps[:])
-        put_v(pw[1], l_pw_put, a1_sb[:])
+        put_v(pw[1], l_pw_put, a_sb[:, 1, :])
         nc.scalar.copy(a_sb[:, 2:4, :], a23_ps[:])
         get_w(0)
         nc.vector.tensor_copy(b_sb[:, 0:2, :], b01_ps[:])
@@ -158,13 +166,13 @@ def tile_list_oneforboth_twoboards_one_finalgate_kernel(
         nc.scalar.copy(b_sb[:, 2:4, :], b23_ps[:])
         put_v(pv[1], l_pv_put, b_sb[:, 1, :])
         put_s(pv[0], l_pv_put, b_sb[:, 0, :])
+        get_w_v(3)
         put_v(pv[3], l_pv_put, b_sb[:, 3, :])
         get_w(1)
+        get_w(2)
         put_s(pv[2], l_pv_put, b_sb[:, 2, :])
         get_diff(0, 0, O)
         get_diff(1, 0, O)
-        get_w(3)
-        get_w(2)
         get_diff(3, 0, O)
         look(0)
         get_diff(2, 0, HALF)
@@ -172,17 +180,21 @@ def tile_list_oneforboth_twoboards_one_finalgate_kernel(
 
         out_v = out.rearrange("(h p) o -> p h o", p=P)
         p_banks = []
-        for u in range(2):
-            cols = slice(u * HALF, (u + 1) * HALF)
-            hid = sb("hid%d" % u, [P, HALF * PACK], BF16, tag="tz0" if u == 0 else None)
+        hid_all = sb("hid_all", [P, 2, HALF * PACK], BF16, tag="tz0")
+        hid_cols = hid_all[:].rearrange("p u (o t) -> p (u o) t", t=PACK)
+        for lo, hi in [(0, HALF), (HALF, 192)]:
             nc.scalar.activation(
-                out=hid[:].rearrange("p (c i t) -> p c t i", i=4, t=PACK),
-                in_=diff[:, :, cols].rearrange("p t (c i) -> p c t i", i=4),
+                out=hid_cols[:, lo:hi, :].rearrange("p (c i) t -> p c t i", i=4),
+                in_=diff[:, :, lo:hi].rearrange("p t (c i) -> p c t i", i=4),
                 func=ACT.Abs,
             )
+        last = diff[:, :, 192:O].rearrange("p t o -> p o t")
+        nc.vector.scalar_tensor_tensor(hid_cols[:, 192:O, :], last, -1.0, last, ALU.mult, ALU.max)
+        for u in range(2):
+            hid = hid_all[:, u, :]
             hid_w = sb("hid_w%d" % u, [P, HALF], U32)
             hid_sc = sb("hid_sc%d" % u, [P, HALF], U8)
-            nc.vector.quantize_mx(out=hid_w[:].bitcast(E5M2), scales=hid_sc[:], in_=hid[:])
+            nc.vector.quantize_mx(out=hid_w[:].bitcast(E5M2), scales=hid_sc[:], in_=hid)
             p_ps = psum.tile([P, 2, HALF], F32, name="p_ps%d" % u)
             for h in range(2):
                 nc.tensor.matmul_mx(

@@ -59,11 +59,11 @@ def tile_list_oneforboth_twoboards_one_finalgate_kernel(
         nc.sync.dma_start(xt_w[:].bitcast(I32), xt_words[0].bitcast(I32))
         for q, queue in [(1, nc.sync), (2, nc.scalar), (3, nc.sync)]:
             load_scale_rows(w_sc, w_scales, q, queue)
-        for q, queue in enumerate([nc.scalar, nc.scalar, nc.gpsimd, nc.gpsimd]):
-            load_scale_rows(xo_sc, xo_scales, q, queue)
-        l_xo = load_list("l_xo", offs2)
         xo_w = sb("xo_w", [P, Z], U32)
-        nc.sync.dma_start(xo_w[:].bitcast(I32), xo_words[0].rearrange("p c t -> p (c t)").bitcast(I32))
+        nc.scalar.dma_start(xo_w[:].bitcast(I32), xo_words[0].rearrange("p c t -> p (c t)").bitcast(I32))
+        l_xo = load_list("l_xo", offs2)
+        for q, queue in enumerate([nc.scalar, nc.sync, nc.gpsimd, nc.gpsimd]):
+            load_scale_rows(xo_sc, xo_scales, q, queue)
         l_pw_put = load_list("l_pw_put", offs3)
         l_pw_get = load_list("l_pw_get", offs5)
         l_pv_put = load_list("l_pv_put", offs4)
@@ -98,7 +98,10 @@ def tile_list_oneforboth_twoboards_one_finalgate_kernel(
         xt_sc_g = sb("xt_sc_g", [P, J], U8)
         nc.vector.tensor_copy(xt_g[:], xt_w[:].indirect(l_xt[:]))
         nc.vector.tensor_copy(xt_sc_g[:], xt_sc[:].indirect(l_xt[:]))
-        nc.vector.tensor_copy(w_sc_deal[:].rearrange("p t m -> p m t"), w_sc[:].rearrange("p (m t) -> p m t", t=PACK))
+        for ts in (slice(0, 2), slice(2, 4)):
+            nc.vector.tensor_copy(
+                w_sc_deal[:, ts, :].rearrange("p t m -> p m t"), w_sc[:].rearrange("p (m t) -> p m t", t=PACK)[:, :, ts]
+            )
 
         gate = sb("gate", [P, 2, O], F32)
 
@@ -161,9 +164,10 @@ def tile_list_oneforboth_twoboards_one_finalgate_kernel(
         nc.scalar.copy(a_sb[:, 2:4, :], a23_ps[:])
         get_w(0)
         nc.vector.tensor_copy(b_sb[:, 0:2, :], b01_ps[:])
+        nc.vector.tensor_copy(b_sb[:, 3, :], b23_ps[:, 1, :])
         put_s(pw[2], l_pw_put, a_sb[:, 2, :])
         put_v(pw[3], l_pw_put, a_sb[:, 3, :])
-        nc.scalar.copy(b_sb[:, 2:4, :], b23_ps[:])
+        nc.scalar.copy(b_sb[:, 2, :], b23_ps[:, 0, :])
         put_v(pv[1], l_pv_put, b_sb[:, 1, :])
         put_s(pv[0], l_pv_put, b_sb[:, 0, :])
         get_w_v(3)
@@ -203,9 +207,13 @@ def tile_list_oneforboth_twoboards_one_finalgate_kernel(
                     rhs=hid_w[:].bitcast(E5M2), rhs_scale=hid_sc[:], start=True, stop=True,
                 )
             p_banks.append(p_ps)
+        first, second = slice(0, HALF), slice(HALF, O)
+        res0 = sb("res0", [P, 2, HALF], F32)
+        res1 = sb("res1", [P, 2, HALF], F32)
+        nc.vector.tensor_tensor(res0[:, 0, :], p_banks[0][:, 0, :], gate[:, 0, first], ALU.mult)
         look(1)
-        for u, p_ps in enumerate(p_banks):
-            cols = slice(u * HALF, (u + 1) * HALF)
-            res = sb("res%d" % u, [P, 2, HALF], F32)
-            nc.vector.tensor_tensor(res[:], p_ps[:], gate[:, :, cols], ALU.mult)
-            nc.sync.dma_start(out_v[:, :, cols], res[:])
+        nc.vector.tensor_tensor(res0[:, 1, :], p_banks[0][:, 1, :], gate[:, 1, first], ALU.mult)
+        nc.sync.dma_start(out_v[:, :, first], res0[:])
+        nc.vector.tensor_tensor(res1[:], p_banks[1][:], gate[:, :, second], ALU.mult)
+        nc.sync.dma_start(out_v[:, 0, second], res1[:, 0, :])
+        nc.scalar.dma_start(out_v[:, 1, second], res1[:, 1, :])

from contextlib import ExitStack

import concourse.mybir as mybir

K, T, Z, J, R, C, O, N, E = 512, 1024, 1024, 256, 512, 512, 256, 256, 1024
FLOPS = 2 * (2 * K * R * J + R * N * O)

F32 = mybir.dt.float32
BF16 = mybir.dt.bfloat16
I32 = mybir.dt.int32
U32 = mybir.dt.uint32
U16 = mybir.dt.uint16
U8 = mybir.dt.uint8
E4M3 = mybir.dt.float8_e4m3fn_x4
E5M2 = mybir.dt.float8_e5m2_x4
E2M1 = mybir.dt.float4_e2m1fn_x4
ACT = mybir.ActivationFunctionType
ALU = mybir.AluOpType

P = 128
PACK = 4
HALF = O // 2


def tile_list_oneforboth_twoboards_one_finalgate_kernel(
    tc, xt_words, xt_scales, xo_words, xo_scales, w_words, w_scales, wb_words, wb_scales,
    tz, so, bo, offs, offs2, offs3, offs4, offs5, offs6, offs7, out,
):
    nc = tc.nc
    with ExitStack() as ctx:
        keep = ctx.enter_context(tc.tile_pool(name="keep", bufs=1))
        psum = ctx.enter_context(tc.psum_pool(name="psum", bufs=1))

        def sb(name, shape, dtype, tag=None):
            return keep.tile(shape, dtype, name=name, tag=tag or name, align_bytes=64)

        def load_list(name, src):
            lst = sb(name, [P, J // 16], U16)
            nc.sync.dma_start(lst[:], src)
            return lst

        def load_scale_rows(plane, src, q, queue):
            rows = src[0, 4 * q : 4 * q + 4, :].bitcast(I32)
            queue.dma_start(
                plane[32 * q : 32 * q + 32, :].bitcast(I32), rows.unsqueeze(0).to_broadcast([8] + list(rows.shape))
            )

        l_xt = load_list("l_xt", offs)
        xt_sc = sb("xt_sc", [P, T], U8)
        w_sc = sb("w_sc", [P, R], U8)
        xo_sc = sb("xo_sc", [P, Z], U8)
        wb_sc = sb("wb_sc", [P, N], U8)
        for q in range(4):
            load_scale_rows(xt_sc, xt_scales, q, nc.scalar)
        load_scale_rows(w_sc, w_scales, 0, nc.sync)
        w_raw = sb("w_raw", [P, R], U32)
        nc.sync.dma_start(w_raw[:].bitcast(I32), w_words[0].rearrange("p c t -> p (c t)").bitcast(I32))
        xt_w = sb("xt_w", [P, T], U16)
        nc.sync.dma_start(xt_w[:].bitcast(I32), xt_words[0].bitcast(I32))
        for q, queue in [(1, nc.sync), (2, nc.scalar), (3, nc.sync)]:
            load_scale_rows(w_sc, w_scales, q, queue)
        xo_w = sb("xo_w", [P, Z], U32)
        nc.scalar.dma_start(xo_w[:].bitcast(I32), xo_words[0].rearrange("p c t -> p (c t)").bitcast(I32))
        l_xo = load_list("l_xo", offs2)
        for q, queue in enumerate([nc.scalar, nc.sync, nc.gpsimd, nc.gpsimd]):
            load_scale_rows(xo_sc, xo_scales, q, queue)
        l_pw_put = load_list("l_pw_put", offs3)
        l_pw_get = load_list("l_pw_get", offs5)
        l_pv_put = load_list("l_pv_put", offs4)
        l_pv_get = load_list("l_pv_get", offs6)
        l_tz = load_list("l_tz", offs7)
        slope = sb("slope", [P, 2], F32)
        offset = sb("offset", [P, 2], F32)
        with nc.allow_non_contiguous_dma(reason="one value a partition"):
            nc.gpsimd.dma_start(slope[:], so.rearrange("(h p) o -> p (h o)", p=P))
            nc.gpsimd.dma_start(offset[:], bo.rearrange("(h p) o -> p (h o)", p=P))
        tz_sb = [sb("tz%d" % h, [P, E], F32) for h in range(2)]
        nc.sync.dma_start(tz_sb[0][:], tz[0:P, :])
        for q in range(4):
            load_scale_rows(wb_sc, wb_scales, q, nc.sync)
        wb_w = sb("wb_w", [P, 2 * N], U8)
        nc.sync.dma_start(wb_w[:].bitcast(I32), wb_words[0].bitcast(I32))
        nc.sync.dma_start(tz_sb[1][:], tz[P : 2 * P, :])

        warm_in = sb("warm_in", [P, 1], F32)
        warm_out = sb("warm_out", [P, 1], F32)
        nc.vector.memset(warm_in[:], 0.0)
        nc.scalar.activation(out=warm_out[:], in_=warm_in[:], func=ACT.Sigmoid)
        pw = [sb("pw%d" % t, [P, C], F32) for t in range(PACK)]
        for board in pw:
            nc.vector.memset(board[:], 0.0)

        w_deal = sb("w_deal", [P, PACK, P], U32)
        w_sc_deal = sb("w_sc_deal", [P, PACK, P], U8)
        nc.vector.tensor_copy(w_deal[:].rearrange("p t m -> p m t"), w_raw[:].rearrange("p (m t) -> p m t", t=PACK))

        xt_g = sb("xt_g", [P, J], U16)
        xt_sc_g = sb("xt_sc_g", [P, J], U8)
        nc.vector.tensor_copy(xt_g[:], xt_w[:].indirect(l_xt[:]))
        nc.vector.tensor_copy(xt_sc_g[:], xt_sc[:].indirect(l_xt[:]))
        for ts in (slice(0, 2), slice(2, 4)):
            nc.vector.tensor_copy(
                w_sc_deal[:, ts, :].rearrange("p t m -> p m t"), w_sc[:].rearrange("p (m t) -> p m t", t=PACK)[:, :, ts]
            )

        gate = sb("gate", [P, 2, O], F32)

        def look(h):
            nc.scalar.activation(
                out=gate[:, h, :], in_=tz_sb[h][:].indirect(l_tz[:]), func=ACT.Sigmoid,
                bias=offset[:, h : h + 1], scale=slope[:, h : h + 1],
            )

        def first_stage(acc, t, words, plane):
            nc.tensor.matmul_mx(
                out=acc, lhsT=w_deal[:, t, :].bitcast(E4M3), lhsT_scale=w_sc_deal[:, t, :],
                rhs=words, rhs_scale=plane[:], start=True, stop=True,
            )

        a0_ps = psum.tile([P, J], F32, name="a0_ps")
        a1_ps = psum.tile([P, J], F32, name="a1_ps")
        a23_ps = psum.tile([P, 2, J], F32, name="a23_ps")
        for t, acc in enumerate([a0_ps[:], a1_ps[:], a23_ps[:, 0, :], a23_ps[:, 1, :]]):
            first_stage(acc, t, xt_g[:].bitcast(E2M1), xt_sc_g)

        xo_g = sb("xo_g", [P, J], U32)
        xo_sc_g = sb("xo_sc_g", [P, J], U8)
        nc.vector.tensor_copy(xo_g[:], xo_w[:].indirect(l_xo[:]))
        nc.vector.tensor_copy(xo_sc_g[:], xo_sc[:].indirect(l_xo[:]))
        b01_ps = psum.tile([P, 2, J], F32, name="b01_ps")
        b23_ps = psum.tile([P, 2, J], F32, name="b23_ps")
        for t, acc in enumerate([b01_ps[:, 0, :], b01_ps[:, 1, :], b23_ps[:, 0, :], b23_ps[:, 1, :]]):
            first_stage(acc, t, xo_g[:].bitcast(E4M3), xo_sc_g)

        a_sb = sb("a_sb", [P, PACK, J], F32)
        b_sb = sb("b_sb", [P, PACK, J], F32)
        got_w = sb("got_w", [P, PACK, O], F32)
        diff = sb("diff", [P, PACK, O], F32)

        def put_s(board, lst, src):
            nc.scalar.activation(out=board[:].indirect(lst[:]), in_=src, func=ACT.Copy)

        def put_v(board, lst, src):
            nc.vector.tensor_copy(board[:].indirect(lst[:]), src)

        def get_w(t):
            nc.scalar.activation(out=got_w[:, t, :], in_=pw[t][:].indirect(l_pw_get[:]), func=ACT.Copy)

        def get_diff(t, lo, hi):
            nc.vector.tensor_tensor(
                diff[:, t, lo:hi], pv[t][:].indirect(l_pv_get[:, lo // 16 : hi // 16]), got_w[:, t, lo:hi], ALU.subtract
            )

        pv = [sb("pv%d" % t, [P, C], F32, tag=tag) for t, tag in enumerate(["xo_w", "w_sc", "xo_sc", "xt_g"])]
        for board in pv:
            nc.gpsimd.memset(board[:], 0.0)
        def get_w_v(t):
            nc.vector.tensor_copy(got_w[:, t, :], pw[t][:].indirect(l_pw_get[:]))

        nc.scalar.copy(a_sb[:, 0, :], a0_ps[:])
        nc.scalar.copy(a_sb[:, 1, :], a1_ps[:])
        put_s(pw[0], l_pw_put, a_sb[:, 0, :])
        put_v(pw[1], l_pw_put, a_sb[:, 1, :])
        nc.scalar.copy(a_sb[:, 2:4, :], a23_ps[:])
        get_w(0)
        nc.vector.tensor_copy(b_sb[:, 0:2, :], b01_ps[:])
        nc.vector.tensor_copy(b_sb[:, 3, :], b23_ps[:, 1, :])
        put_s(pw[2], l_pw_put, a_sb[:, 2, :])
        put_v(pw[3], l_pw_put, a_sb[:, 3, :])
        nc.scalar.copy(b_sb[:, 2, :], b23_ps[:, 0, :])
        put_v(pv[1], l_pv_put, b_sb[:, 1, :])
        put_s(pv[0], l_pv_put, b_sb[:, 0, :])
        get_w_v(3)
        put_v(pv[3], l_pv_put, b_sb[:, 3, :])
        get_w(1)
        get_w(2)
        put_s(pv[2], l_pv_put, b_sb[:, 2, :])
        get_diff(0, 0, O)
        get_diff(1, 0, O)
        get_diff(3, 0, O)
        look(0)
        get_diff(2, 0, HALF)
        get_diff(2, HALF, O)

        out_v = out.rearrange("(h p) o -> p h o", p=P)
        p_banks = []
        hid_all = sb("hid_all", [P, 2, HALF * PACK], BF16, tag="tz0")
        hid_cols = hid_all[:].rearrange("p u (o t) -> p (u o) t", t=PACK)
        for lo, hi in [(0, HALF), (HALF, 192)]:
            nc.scalar.activation(
                out=hid_cols[:, lo:hi, :].rearrange("p (c i) t -> p c t i", i=4),
                in_=diff[:, :, lo:hi].rearrange("p t (c i) -> p c t i", i=4),
                func=ACT.Abs,
            )
        last = diff[:, :, 192:O].rearrange("p t o -> p o t")
        nc.vector.scalar_tensor_tensor(hid_cols[:, 192:O, :], last, -1.0, last, ALU.mult, ALU.max)
        for u in range(2):
            hid = hid_all[:, u, :]
            hid_w = sb("hid_w%d" % u, [P, HALF], U32)
            hid_sc = sb("hid_sc%d" % u, [P, HALF], U8)
            nc.vector.quantize_mx(out=hid_w[:].bitcast(E5M2), scales=hid_sc[:], in_=hid)
            p_ps = psum.tile([P, 2, HALF], F32, name="p_ps%d" % u)
            for h in range(2):
                nc.tensor.matmul_mx(
                    out=p_ps[:, h, :], lhsT=wb_w[:, 2 * P * h : 2 * P * (h + 1)].bitcast(E2M1),
                    lhsT_scale=wb_sc[:, P * h : P * (h + 1)],
                    rhs=hid_w[:].bitcast(E5M2), rhs_scale=hid_sc[:], start=True, stop=True,
                )
            p_banks.append(p_ps)
        first, second = slice(0, HALF), slice(HALF, O)
        res0 = sb("res0", [P, 2, HALF], F32)
        res1 = sb("res1", [P, 2, HALF], F32)
        nc.vector.tensor_tensor(res0[:, 0, :], p_banks[0][:, 0, :], gate[:, 0, first], ALU.mult)
        look(1)
        nc.vector.tensor_tensor(res0[:, 1, :], p_banks[0][:, 1, :], gate[:, 1, first], ALU.mult)
        nc.sync.dma_start(out_v[:, :, first], res0[:])
        nc.vector.tensor_tensor(res1[:], p_banks[1][:], gate[:, :, second], ALU.mult)
        nc.sync.dma_start(out_v[:, 0, second], res1[:, 0, :])
        nc.scalar.dma_start(out_v[:, 1, second], res1[:, 1, :])
